import numpy as np
import ml_dtypes

BF16 = ml_dtypes.bfloat16


def bf(x):
    return np.asarray(x, np.float32).astype(BF16)


def f32(x):
    return np.asarray(x, np.float32)


def f64(x):
    return np.asarray(x).astype(np.float64)


def striped(idx):
    return np.tile(idx.reshape(-1, 16).T, (8, 1))


def rows(idx, k):
    return np.tile(idx, (k, 1))


def look(tab, idx):
    return np.take_along_axis(f64(tab), rows(idx, len(tab)), axis=1)


K, S, V, N = 512, 2048, 512, 512


def setup_inputs():
    return {"tab": f32(np.random.standard_normal((2, K, S))), "y": f32(np.random.standard_normal((K, V))), "offs": striped(np.random.permutation(S)[:N])}


def reference(tab, y, offs):
    idx = offs[:16].T.reshape(-1)
    x = (np.minimum(look(tab[0], idx), f64(y))) * (np.maximum(look(tab[1], idx), 0.0))
    return x

@@ -1,0 +1,46 @@
+import concourse.mybir as mybir
+
+F32, U16 = mybir.dt.float32, mybir.dt.uint16
+MIN, MULT = mybir.AluOpType.min, mybir.AluOpType.mult
+RELU = mybir.ActivationFunctionType.Relu
+P = 128
+
+
+def tile_lookup_vg_minrelu_out_kernel(tc, tab, y, offs, out):
+    nc = tc.nc
+    rows, entries = y.shape
+    places = tab.shape[2]
+    blocks = rows // P
+    tab_rows = tab.rearrange("t (p b) s -> t p b s", b=blocks)
+    y_rows = y.rearrange("(p b) j -> p (b j)", b=blocks)
+    out_rows = out.rearrange("(p b) j -> p b j", b=blocks)
+    with tc.tile_pool(name="held", bufs=1) as held:
+        offsets = held.tile([P, entries // 16], U16, name="offsets")
+        nc.sync.dma_start(offsets[:], offs)
+
+        stream = held.tile([P, blocks * entries], F32, name="stream")
+        nc.sync.dma_start(stream[:], y_rows)
+        values, gates = [], []
+        for b in range(blocks):
+            value = held.tile([P, places], F32, name=f"value{b}")
+            nc.scalar.dma_start(value[:], tab_rows[0, :, b, :])
+            gate = held.tile([P, places], F32, name=f"gate{b}")
+            nc.sync.dma_start(gate[:], tab_rows[1, :, b, :])
+            values.append(value)
+            gates.append(gate)
+
+        for b in range(blocks):
+            pieces = 2 if b == blocks - 1 else 1
+            width = entries // pieces
+            capped = held.tile([P, entries], F32, name=f"capped{b}")
+            nc.vector.tensor_tensor(
+                capped[:], values[b][:].indirect(offsets[:]), stream[:, b * entries : (b + 1) * entries], MIN
+            )
+            for i in range(pieces):
+                piece = slice(i * width, (i + 1) * width)
+                listed = offsets[:, i * width // 16 : (i + 1) * width // 16]
+                opened = held.tile([P, width], F32, name=f"opened{b}_{i}")
+                nc.scalar.activation(opened[:], gates[b][:].indirect(listed), RELU)
+                product = held.tile([P, width], F32, name=f"product{b}_{i}")
+                nc.vector.tensor_tensor(product[:], capped[:, piece], opened[:], MULT)
+                nc.sync.dma_start(out_rows[:, b, piece], product[:])

@@ -11,23 +11,32 @@ def tile_lookup_vg_minrelu_out_kernel(tc, tab, y, offs, out):
     rows, entries = y.shape
     places = tab.shape[2]
     blocks = rows // P
-    tab_rows = tab.rearrange("t (p b) s -> t p b s", b=blocks)
+    value_rows = tab[0].rearrange("(p b) s -> p (b s)", b=blocks)
+    gate_rows = tab[1].rearrange("(p b) s -> p b s", b=blocks)
     y_rows = y.rearrange("(p b) j -> p (b j)", b=blocks)
     out_rows = out.rearrange("(p b) j -> p b j", b=blocks)
     with tc.tile_pool(name="held", bufs=1) as held:
         offsets = held.tile([P, entries // 16], U16, name="offsets")
         nc.sync.dma_start(offsets[:], offs)
 
+        all_values = held.tile([P, blocks * places], F32, name="all_values")
+        nc.sync.dma_start(all_values[:], value_rows)
         stream = held.tile([P, blocks * entries], F32, name="stream")
         nc.sync.dma_start(stream[:], y_rows)
-        values, gates = [], []
+        gates = []
+        for b in range(blocks):
+            gate = held.tile([P, places], F32, name=f"gate{b}")
+            nc.sync.dma_start(gate[:], gate_rows[:, b, :])
+            gates.append(gate)
+
+        values = []
         for b in range(blocks):
             value = held.tile([P, places], F32, name=f"value{b}")
-            nc.scalar.dma_start(value[:], tab_rows[0, :, b, :])
-            gate = held.tile([P, places], F32, name=f"gate{b}")
-            nc.sync.dma_start(gate[:], tab_rows[1, :, b, :])
+            if b < blocks // 2:
+                nc.vector.tensor_copy(value[:], all_values[:, b * places : (b + 1) * places])
+            else:
+                nc.scalar.copy(value[:], all_values[:, b * places : (b + 1) * places])
             values.append(value)
-            gates.append(gate)
 
         for b in range(blocks):
             pieces = 2 if b == blocks - 1 else 1

@@ -11,23 +11,29 @@ def tile_lookup_vg_minrelu_out_kernel(tc, tab, y, offs, out):
     rows, entries = y.shape
     places = tab.shape[2]
     blocks = rows // P
+    last = blocks - 1
+    half = entries // 2
     value_rows = tab[0].rearrange("(p b) s -> p (b s)", b=blocks)
     gate_rows = tab[1].rearrange("(p b) s -> p b s", b=blocks)
     y_rows = y.rearrange("(p b) j -> p (b j)", b=blocks)
     out_rows = out.rearrange("(p b) j -> p b j", b=blocks)
     with tc.tile_pool(name="held", bufs=1) as held:
-        offsets = held.tile([P, entries // 16], U16, name="offsets")
-        nc.sync.dma_start(offsets[:], offs)
-
         all_values = held.tile([P, blocks * places], F32, name="all_values")
         nc.sync.dma_start(all_values[:], value_rows)
-        stream = held.tile([P, blocks * entries], F32, name="stream")
-        nc.sync.dma_start(stream[:], y_rows)
+        offsets = held.tile([P, entries // 16], U16, name="offsets")
+        nc.sync.dma_start(offsets[:], offs)
+        stream = held.tile([P, blocks * entries - half], F32, name="stream")
+        nc.sync.dma_start(stream[:], y_rows[:, : blocks * entries - half])
         gates = []
         for b in range(blocks):
             gate = held.tile([P, places], F32, name=f"gate{b}")
             nc.sync.dma_start(gate[:], gate_rows[:, b, :])
             gates.append(gate)
+        stream_end = held.tile([P, half], F32, name="stream_end")
+        nc.sync.dma_start(stream_end[:], y_rows[:, blocks * entries - half :])
+
+        def listed(first, end):
+            return offsets[:, first // 16 : end // 16]
 
         values = []
         for b in range(blocks):
@@ -39,17 +45,22 @@ def tile_lookup_vg_minrelu_out_kernel(tc, tab, y, offs, out):
             values.append(value)
 
         for b in range(blocks):
-            pieces = 2 if b == blocks - 1 else 1
-            width = entries // pieces
+            early = half if b == last else entries
             capped = held.tile([P, entries], F32, name=f"capped{b}")
             nc.vector.tensor_tensor(
-                capped[:], values[b][:].indirect(offsets[:]), stream[:, b * entries : (b + 1) * entries], MIN
+                capped[:, :early], values[b][:].indirect(listed(0, early)),
+                stream[:, b * entries : b * entries + early], MIN,
             )
-            for i in range(pieces):
-                piece = slice(i * width, (i + 1) * width)
-                listed = offsets[:, i * width // 16 : (i + 1) * width // 16]
-                opened = held.tile([P, width], F32, name=f"opened{b}_{i}")
-                nc.scalar.activation(opened[:], gates[b][:].indirect(listed), RELU)
-                product = held.tile([P, width], F32, name=f"product{b}_{i}")
-                nc.vector.tensor_tensor(product[:], capped[:, piece], opened[:], MULT)
-                nc.sync.dma_start(out_rows[:, b, piece], product[:])
+            if b == last:
+                nc.vector.tensor_tensor(
+                    capped[:, early:], values[b][:].indirect(listed(early, entries)), stream_end[:], MIN
+                )
+            for first, end in [(0, half), (half, entries)] if b == last else [(0, entries)]:
+                opened = held.tile([P, end - first], F32, name=f"opened{b}_{first}")
+                nc.scalar.activation(opened[:], gates[b][:].indirect(listed(first, end)), RELU)
+                if b == last and first == 0:
+                    product = stream_end
+                else:
+                    product = held.tile([P, end - first], F32, name=f"product{b}_{first}")
+                nc.vector.tensor_tensor(product[:], capped[:, first:end], opened[:], MULT)
+                nc.sync.dma_start(out_rows[:, b, first:end], product[:])

@@ -18,10 +18,10 @@ def tile_lookup_vg_minrelu_out_kernel(tc, tab, y, offs, out):
     y_rows = y.rearrange("(p b) j -> p (b j)", b=blocks)
     out_rows = out.rearrange("(p b) j -> p b j", b=blocks)
     with tc.tile_pool(name="held", bufs=1) as held:
-        all_values = held.tile([P, blocks * places], F32, name="all_values")
-        nc.sync.dma_start(all_values[:], value_rows)
         offsets = held.tile([P, entries // 16], U16, name="offsets")
         nc.sync.dma_start(offsets[:], offs)
+        all_values = held.tile([P, blocks * places], F32, name="all_values")
+        nc.sync.dma_start(all_values[:], value_rows)
         stream = held.tile([P, blocks * entries - half], F32, name="stream")
         nc.sync.dma_start(stream[:], y_rows[:, : blocks * entries - half])
         gates = []

@@ -21,13 +21,14 @@ def tile_lookup_vg_minrelu_out_kernel(tc, tab, y, offs, out):
         offsets = held.tile([P, entries // 16], U16, name="offsets")
         nc.sync.dma_start(offsets[:], offs)
         all_values = held.tile([P, blocks * places], F32, name="all_values")
-        nc.sync.dma_start(all_values[:], value_rows)
+        nc.scalar.dma_start(all_values[:, : 2 * places], value_rows[:, : 2 * places])
+        nc.sync.dma_start(all_values[:, 2 * places :], value_rows[:, 2 * places :])
         stream = held.tile([P, blocks * entries - half], F32, name="stream")
         nc.sync.dma_start(stream[:], y_rows[:, : blocks * entries - half])
         gates = []
         for b in range(blocks):
             gate = held.tile([P, places], F32, name=f"gate{b}")
-            nc.sync.dma_start(gate[:], gate_rows[:, b, :])
+            (nc.scalar if b == 0 else nc.sync).dma_start(gate[:], gate_rows[:, b, :])
             gates.append(gate)
         stream_end = held.tile([P, half], F32, name="stream_end")
         nc.sync.dma_start(stream_end[:], y_rows[:, blocks * entries - half :])

@@ -18,11 +18,11 @@ def tile_lookup_vg_minrelu_out_kernel(tc, tab, y, offs, out):
     y_rows = y.rearrange("(p b) j -> p (b j)", b=blocks)
     out_rows = out.rearrange("(p b) j -> p b j", b=blocks)
     with tc.tile_pool(name="held", bufs=1) as held:
-        offsets = held.tile([P, entries // 16], U16, name="offsets")
-        nc.sync.dma_start(offsets[:], offs)
         all_values = held.tile([P, blocks * places], F32, name="all_values")
         nc.scalar.dma_start(all_values[:, : 2 * places], value_rows[:, : 2 * places])
         nc.sync.dma_start(all_values[:, 2 * places :], value_rows[:, 2 * places :])
+        offsets = held.tile([P, entries // 16], U16, name="offsets")
+        nc.sync.dma_start(offsets[:], offs)
         stream = held.tile([P, blocks * entries - half], F32, name="stream")
         nc.sync.dma_start(stream[:], y_rows[:, : blocks * entries - half])
         gates = []
@@ -57,11 +57,15 @@ def tile_lookup_vg_minrelu_out_kernel(tc, tab, y, offs, out):
                     capped[:, early:], values[b][:].indirect(listed(early, entries)), stream_end[:], MIN
                 )
             for first, end in [(0, half), (half, entries)] if b == last else [(0, entries)]:
-                opened = held.tile([P, end - first], F32, name=f"opened{b}_{first}")
-                nc.scalar.activation(opened[:], gates[b][:].indirect(listed(first, end)), RELU)
                 if b == last and first == 0:
                     product = stream_end
                 else:
                     product = held.tile([P, end - first], F32, name=f"product{b}_{first}")
-                nc.vector.tensor_tensor(product[:], capped[:, first:end], opened[:], MULT)
+                step = (end - first) // 2 if b == last and first == half else end - first
+                for start in range(first, end, step):
+                    opened = held.tile([P, step], F32, name=f"opened{b}_{start}")
+                    nc.scalar.activation(opened[:], gates[b][:].indirect(listed(start, start + step)), RELU)
+                    nc.vector.tensor_tensor(
+                        product[:, start - first : start - first + step], capped[:, start : start + step], opened[:], MULT
+                    )
                 nc.sync.dma_start(out_rows[:, b, first:end], product[:])

@@ -13,25 +13,25 @@ def tile_lookup_vg_minrelu_out_kernel(tc, tab, y, offs, out):
     blocks = rows // P
     last = blocks - 1
     half = entries // 2
+    lead = entries // 8
     value_rows = tab[0].rearrange("(p b) s -> p (b s)", b=blocks)
     gate_rows = tab[1].rearrange("(p b) s -> p b s", b=blocks)
     y_rows = y.rearrange("(p b) j -> p (b j)", b=blocks)
     out_rows = out.rearrange("(p b) j -> p b j", b=blocks)
     with tc.tile_pool(name="held", bufs=1) as held:
         all_values = held.tile([P, blocks * places], F32, name="all_values")
-        nc.scalar.dma_start(all_values[:, : 2 * places], value_rows[:, : 2 * places])
-        nc.sync.dma_start(all_values[:, 2 * places :], value_rows[:, 2 * places :])
+        nc.sync.dma_start(all_values[:], value_rows)
         offsets = held.tile([P, entries // 16], U16, name="offsets")
         nc.sync.dma_start(offsets[:], offs)
         stream = held.tile([P, blocks * entries - half], F32, name="stream")
-        nc.sync.dma_start(stream[:], y_rows[:, : blocks * entries - half])
+        nc.scalar.dma_start(stream[:], y_rows[:, : blocks * entries - half])
         gates = []
         for b in range(blocks):
             gate = held.tile([P, places], F32, name=f"gate{b}")
-            (nc.scalar if b == 0 else nc.sync).dma_start(gate[:], gate_rows[:, b, :])
+            nc.sync.dma_start(gate[:], gate_rows[:, b, :])
             gates.append(gate)
-        stream_end = held.tile([P, half], F32, name="stream_end")
-        nc.sync.dma_start(stream_end[:], y_rows[:, blocks * entries - half :])
+        stream_end = held.tile([P, entries - lead], F32, name="stream_end")
+        nc.sync.dma_start(stream_end[:, half - lead :], y_rows[:, blocks * entries - half :])
 
         def listed(first, end):
             return offsets[:, first // 16 : end // 16]
@@ -53,9 +53,11 @@ def tile_lookup_vg_minrelu_out_kernel(tc, tab, y, offs, out):
                 stream[:, b * entries : b * entries + early], MIN,
             )
             if b == last:
-                nc.vector.tensor_tensor(
-                    capped[:, early:], values[b][:].indirect(listed(early, entries)), stream_end[:], MIN
-                )
+                for start, end in [(early, early + lead), (early + lead, entries)]:
+                    nc.vector.tensor_tensor(
+                        capped[:, start:end], values[b][:].indirect(listed(start, end)),
+                        stream_end[:, half + start - early - lead : half + end - early - lead], MIN,
+                    )
             for first, end in [(0, half), (half, entries)] if b == last else [(0, entries)]:
                 if b == last and first == 0:
                     product = stream_end
@@ -68,4 +70,4 @@ def tile_lookup_vg_minrelu_out_kernel(tc, tab, y, offs, out):
                     nc.vector.tensor_tensor(
                         product[:, start - first : start - first + step], capped[:, start : start + step], opened[:], MULT
                     )
-                nc.sync.dma_start(out_rows[:, b, first:end], product[:])
+                nc.sync.dma_start(out_rows[:, b, first:end], product[:, : end - first])

@@ -28,7 +28,7 @@ def tile_lookup_vg_minrelu_out_kernel(tc, tab, y, offs, out):
         gates = []
         for b in range(blocks):
             gate = held.tile([P, places], F32, name=f"gate{b}")
-            nc.sync.dma_start(gate[:], gate_rows[:, b, :])
+            (nc.scalar if b == 0 else nc.sync).dma_start(gate[:], gate_rows[:, b, :])
             gates.append(gate)
         stream_end = held.tile([P, entries - lead], F32, name="stream_end")
         nc.sync.dma_start(stream_end[:, half - lead :], y_rows[:, blocks * entries - half :])

@@ -4,6 +4,7 @@ F32, U16 = mybir.dt.float32, mybir.dt.uint16
 MIN, MULT = mybir.AluOpType.min, mybir.AluOpType.mult
 RELU = mybir.ActivationFunctionType.Relu
 P = 128
+STEP = 64
 
 
 def tile_lookup_vg_minrelu_out_kernel(tc, tab, y, offs, out):
@@ -13,7 +14,6 @@ def tile_lookup_vg_minrelu_out_kernel(tc, tab, y, offs, out):
     blocks = rows // P
     last = blocks - 1
     half = entries // 2
-    lead = entries // 8
     value_rows = tab[0].rearrange("(p b) s -> p (b s)", b=blocks)
     gate_rows = tab[1].rearrange("(p b) s -> p b s", b=blocks)
     y_rows = y.rearrange("(p b) j -> p (b j)", b=blocks)
@@ -30,8 +30,9 @@ def tile_lookup_vg_minrelu_out_kernel(tc, tab, y, offs, out):
             gate = held.tile([P, places], F32, name=f"gate{b}")
             (nc.scalar if b == 0 else nc.sync).dma_start(gate[:], gate_rows[:, b, :])
             gates.append(gate)
-        stream_end = held.tile([P, entries - lead], F32, name="stream_end")
-        nc.sync.dma_start(stream_end[:, half - lead :], y_rows[:, blocks * entries - half :])
+        stream_end = held.tile([P, entries - STEP], F32, name="stream_end")
+        late = stream_end[:, half - STEP :]
+        nc.sync.dma_start(late, y_rows[:, blocks * entries - half :])
 
         def listed(first, end):
             return offsets[:, first // 16 : end // 16]
@@ -45,29 +46,30 @@ def tile_lookup_vg_minrelu_out_kernel(tc, tab, y, offs, out):
                 nc.scalar.copy(value[:], all_values[:, b * places : (b + 1) * places])
             values.append(value)
 
-        for b in range(blocks):
-            early = half if b == last else entries
-            capped = held.tile([P, entries], F32, name=f"capped{b}")
-            nc.vector.tensor_tensor(
-                capped[:, :early], values[b][:].indirect(listed(0, early)),
-                stream[:, b * entries : b * entries + early], MIN,
-            )
-            if b == last:
-                for start, end in [(early, early + lead), (early + lead, entries)]:
-                    nc.vector.tensor_tensor(
-                        capped[:, start:end], values[b][:].indirect(listed(start, end)),
-                        stream_end[:, half + start - early - lead : half + end - early - lead], MIN,
-                    )
-            for first, end in [(0, half), (half, entries)] if b == last else [(0, entries)]:
-                if b == last and first == 0:
-                    product = stream_end
-                else:
-                    product = held.tile([P, end - first], F32, name=f"product{b}_{first}")
-                step = (end - first) // 2 if b == last and first == half else end - first
-                for start in range(first, end, step):
-                    opened = held.tile([P, step], F32, name=f"opened{b}_{start}")
-                    nc.scalar.activation(opened[:], gates[b][:].indirect(listed(start, start + step)), RELU)
-                    nc.vector.tensor_tensor(
-                        product[:, start - first : start - first + step], capped[:, start : start + step], opened[:], MULT
-                    )
-                nc.sync.dma_start(out_rows[:, b, first:end], product[:, : end - first])
+        def cap(b, capped, first, end, y_piece):
+            nc.vector.tensor_tensor(capped[:, first:end], values[b][:].indirect(listed(first, end)), y_piece, MIN)
+
+        def gate_and_multiply(b, capped, product, first, end):
+            opened = held.tile([P, end - first], F32, name=f"opened{b}_{first}")
+            nc.scalar.activation(opened[:], gates[b][:].indirect(listed(first, end)), RELU)
+            nc.vector.tensor_tensor(product[:, first:end], capped[:, first:end], opened[:], MULT)
+
+        cappeds = [held.tile([P, entries], F32, name=f"capped{b}") for b in range(blocks)]
+        for b in range(last):
+            cap(b, cappeds[b], 0, entries, stream[:, b * entries : (b + 1) * entries])
+        cap(last, cappeds[last], 0, half, stream[:, last * entries :])
+        for b in range(last):
+            product = held.tile([P, entries], F32, name=f"product{b}")
+            gate_and_multiply(b, cappeds[b], product, 0, entries)
+            nc.sync.dma_start(out_rows[:, b, :], product[:])
+
+        capped = cappeds[last]
+        cap(last, capped, half, half + STEP, late[:, :STEP])
+        cap(last, capped, half + STEP, entries, late[:, STEP:])
+        gate_and_multiply(last, capped, stream_end, 0, half)
+        nc.sync.dma_start(out_rows[:, last, :half], stream_end[:, :half])
+        product = held.tile([P, entries], F32, name="product_last")
+        quarter = half // 2
+        gate_and_multiply(last, capped, product, half, half + quarter)
+        gate_and_multiply(last, capped, product, half + quarter, entries)
+        nc.sync.dma_start(out_rows[:, last, half:], product[:, half:])

@@ -4,6 +4,7 @@ F32, U16 = mybir.dt.float32, mybir.dt.uint16
 MIN, MULT = mybir.AluOpType.min, mybir.AluOpType.mult
 RELU = mybir.ActivationFunctionType.Relu
 P = 128
+ALIGN = 256
 STEP = 64
 
 
@@ -19,18 +20,18 @@ def tile_lookup_vg_minrelu_out_kernel(tc, tab, y, offs, out):
     y_rows = y.rearrange("(p b) j -> p (b j)", b=blocks)
     out_rows = out.rearrange("(p b) j -> p b j", b=blocks)
     with tc.tile_pool(name="held", bufs=1) as held:
-        all_values = held.tile([P, blocks * places], F32, name="all_values")
+        all_values = held.tile([P, blocks * places], F32, name="all_values", align_bytes=ALIGN)
         nc.sync.dma_start(all_values[:], value_rows)
         offsets = held.tile([P, entries // 16], U16, name="offsets")
         nc.sync.dma_start(offsets[:], offs)
-        stream = held.tile([P, blocks * entries - half], F32, name="stream")
+        stream = held.tile([P, blocks * entries - half], F32, name="stream", align_bytes=ALIGN)
         nc.scalar.dma_start(stream[:], y_rows[:, : blocks * entries - half])
         gates = []
         for b in range(blocks):
-            gate = held.tile([P, places], F32, name=f"gate{b}")
-            (nc.scalar if b == 0 else nc.sync).dma_start(gate[:], gate_rows[:, b, :])
+            gate = held.tile([P, places], F32, name=f"gate{b}", align_bytes=ALIGN)
+            nc.sync.dma_start(gate[:], gate_rows[:, b, :])
             gates.append(gate)
-        stream_end = held.tile([P, entries - STEP], F32, name="stream_end")
+        stream_end = held.tile([P, entries - STEP], F32, name="stream_end", align_bytes=ALIGN)
         late = stream_end[:, half - STEP :]
         nc.sync.dma_start(late, y_rows[:, blocks * entries - half :])
 
@@ -39,7 +40,7 @@ def tile_lookup_vg_minrelu_out_kernel(tc, tab, y, offs, out):
 
         values = []
         for b in range(blocks):
-            value = held.tile([P, places], F32, name=f"value{b}")
+            value = held.tile([P, places], F32, name=f"value{b}", align_bytes=ALIGN)
             if b < blocks // 2:
                 nc.vector.tensor_copy(value[:], all_values[:, b * places : (b + 1) * places])
             else:
@@ -50,16 +51,16 @@ def tile_lookup_vg_minrelu_out_kernel(tc, tab, y, offs, out):
             nc.vector.tensor_tensor(capped[:, first:end], values[b][:].indirect(listed(first, end)), y_piece, MIN)
 
         def gate_and_multiply(b, capped, product, first, end):
-            opened = held.tile([P, end - first], F32, name=f"opened{b}_{first}")
+            opened = held.tile([P, end - first], F32, name=f"opened{b}_{first}", align_bytes=ALIGN)
             nc.scalar.activation(opened[:], gates[b][:].indirect(listed(first, end)), RELU)
             nc.vector.tensor_tensor(product[:, first:end], capped[:, first:end], opened[:], MULT)
 
-        cappeds = [held.tile([P, entries], F32, name=f"capped{b}") for b in range(blocks)]
+        cappeds = [held.tile([P, entries], F32, name=f"capped{b}", align_bytes=ALIGN) for b in range(blocks)]
         for b in range(last):
             cap(b, cappeds[b], 0, entries, stream[:, b * entries : (b + 1) * entries])
         cap(last, cappeds[last], 0, half, stream[:, last * entries :])
         for b in range(last):
-            product = held.tile([P, entries], F32, name=f"product{b}")
+            product = held.tile([P, entries], F32, name=f"product{b}", align_bytes=ALIGN)
             gate_and_multiply(b, cappeds[b], product, 0, entries)
             nc.sync.dma_start(out_rows[:, b, :], product[:])
 
@@ -68,7 +69,7 @@ def tile_lookup_vg_minrelu_out_kernel(tc, tab, y, offs, out):
         cap(last, capped, half + STEP, entries, late[:, STEP:])
         gate_and_multiply(last, capped, stream_end, 0, half)
         nc.sync.dma_start(out_rows[:, last, :half], stream_end[:, :half])
-        product = held.tile([P, entries], F32, name="product_last")
+        product = held.tile([P, entries], F32, name="product_last", align_bytes=ALIGN)
         quarter = half // 2
         gate_and_multiply(last, capped, product, half, half + quarter)
         gate_and_multiply(last, capped, product, half + quarter, entries)

@@ -20,57 +20,59 @@ def tile_lookup_vg_minrelu_out_kernel(tc, tab, y, offs, out):
     y_rows = y.rearrange("(p b) j -> p (b j)", b=blocks)
     out_rows = out.rearrange("(p b) j -> p b j", b=blocks)
     with tc.tile_pool(name="held", bufs=1) as held:
-        all_values = held.tile([P, blocks * places], F32, name="all_values", align_bytes=ALIGN)
+
+        def tile(columns, name):
+            return held.tile([P, columns], F32, name=name, align_bytes=ALIGN)
+
+        all_values = tile(blocks * places, "all_values")
         nc.sync.dma_start(all_values[:], value_rows)
         offsets = held.tile([P, entries // 16], U16, name="offsets")
         nc.sync.dma_start(offsets[:], offs)
-        stream = held.tile([P, blocks * entries - half], F32, name="stream", align_bytes=ALIGN)
+        stream = tile(blocks * entries - half, "stream")
         nc.scalar.dma_start(stream[:], y_rows[:, : blocks * entries - half])
-        gates = []
+        gates = [tile(places, f"gate{b}") for b in range(blocks)]
         for b in range(blocks):
-            gate = held.tile([P, places], F32, name=f"gate{b}", align_bytes=ALIGN)
-            nc.sync.dma_start(gate[:], gate_rows[:, b, :])
-            gates.append(gate)
-        stream_end = held.tile([P, entries - STEP], F32, name="stream_end", align_bytes=ALIGN)
+            nc.sync.dma_start(gates[b][:], gate_rows[:, b, :])
+        stream_end = tile(entries - STEP, "stream_end")
         late = stream_end[:, half - STEP :]
         nc.sync.dma_start(late, y_rows[:, blocks * entries - half :])
 
         def listed(first, end):
             return offsets[:, first // 16 : end // 16]
 
-        values = []
+        values = [tile(places, f"value{b}") for b in range(blocks)]
         for b in range(blocks):
-            value = held.tile([P, places], F32, name=f"value{b}", align_bytes=ALIGN)
             if b < blocks // 2:
-                nc.vector.tensor_copy(value[:], all_values[:, b * places : (b + 1) * places])
+                nc.vector.tensor_copy(values[b][:], all_values[:, b * places : (b + 1) * places])
             else:
-                nc.scalar.copy(value[:], all_values[:, b * places : (b + 1) * places])
-            values.append(value)
+                nc.scalar.copy(values[b][:], all_values[:, b * places : (b + 1) * places])
 
         def cap(b, capped, first, end, y_piece):
             nc.vector.tensor_tensor(capped[:, first:end], values[b][:].indirect(listed(first, end)), y_piece, MIN)
 
         def gate_and_multiply(b, capped, product, first, end):
-            opened = held.tile([P, end - first], F32, name=f"opened{b}_{first}", align_bytes=ALIGN)
+            opened = tile(end - first, f"opened{b}_{first}")
             nc.scalar.activation(opened[:], gates[b][:].indirect(listed(first, end)), RELU)
             nc.vector.tensor_tensor(product[:, first:end], capped[:, first:end], opened[:], MULT)
 
-        cappeds = [held.tile([P, entries], F32, name=f"capped{b}", align_bytes=ALIGN) for b in range(blocks)]
+        cappeds = [tile(entries, f"capped{b}") for b in range(blocks)]
         for b in range(last):
             cap(b, cappeds[b], 0, entries, stream[:, b * entries : (b + 1) * entries])
         cap(last, cappeds[last], 0, half, stream[:, last * entries :])
         for b in range(last):
-            product = held.tile([P, entries], F32, name=f"product{b}", align_bytes=ALIGN)
-            gate_and_multiply(b, cappeds[b], product, 0, entries)
-            nc.sync.dma_start(out_rows[:, b, :], product[:])
+            product = tile(entries, f"product{b}")
+            for first, end in [(0, half), (half, entries)] if b == last - 1 else [(0, entries)]:
+                gate_and_multiply(b, cappeds[b], product, first, end)
+                nc.sync.dma_start(out_rows[:, b, first:end], product[:, first:end])
 
-        capped = cappeds[last]
+        capped, product = cappeds[last], tile(entries, "product_last")
         cap(last, capped, half, half + STEP, late[:, :STEP])
         cap(last, capped, half + STEP, entries, late[:, STEP:])
         gate_and_multiply(last, capped, stream_end, 0, half)
         nc.sync.dma_start(out_rows[:, last, :half], stream_end[:, :half])
-        product = held.tile([P, entries], F32, name="product_last", align_bytes=ALIGN)
-        quarter = half // 2
-        gate_and_multiply(last, capped, product, half, half + quarter)
-        gate_and_multiply(last, capped, product, half + quarter, entries)
-        nc.sync.dma_start(out_rows[:, last, half:], product[:, half:])
+        cut = half + half // 2
+        gate_and_multiply(last, capped, product, half, cut)
+        nc.sync.dma_start(out_rows[:, last, half:cut], product[:, half:cut])
+        gate_and_multiply(last, capped, product, cut, entries - STEP)
+        gate_and_multiply(last, capped, product, entries - STEP, entries)
+        nc.sync.dma_start(out_rows[:, last, cut:], product[:, cut:])

@@ -73,6 +73,5 @@ def tile_lookup_vg_minrelu_out_kernel(tc, tab, y, offs, out):
         cut = half + half // 2
         gate_and_multiply(last, capped, product, half, cut)
         nc.sync.dma_start(out_rows[:, last, half:cut], product[:, half:cut])
-        gate_and_multiply(last, capped, product, cut, entries - STEP)
-        gate_and_multiply(last, capped, product, entries - STEP, entries)
+        gate_and_multiply(last, capped, product, cut, entries)
         nc.sync.dma_start(out_rows[:, last, cut:], product[:, cut:])

@@ -18,7 +18,7 @@ def tile_lookup_vg_minrelu_out_kernel(tc, tab, y, offs, out):
     value_rows = tab[0].rearrange("(p b) s -> p (b s)", b=blocks)
     gate_rows = tab[1].rearrange("(p b) s -> p b s", b=blocks)
     y_rows = y.rearrange("(p b) j -> p (b j)", b=blocks)
-    out_rows = out.rearrange("(p b) j -> p b j", b=blocks)
+    out_rows = out.rearrange("(p b) j -> p (b j)", b=blocks)
     with tc.tile_pool(name="held", bufs=1) as held:
 
         def tile(columns, name):
@@ -29,7 +29,7 @@ def tile_lookup_vg_minrelu_out_kernel(tc, tab, y, offs, out):
         offsets = held.tile([P, entries // 16], U16, name="offsets")
         nc.sync.dma_start(offsets[:], offs)
         stream = tile(blocks * entries - half, "stream")
-        nc.scalar.dma_start(stream[:], y_rows[:, : blocks * entries - half])
+        nc.scalar.dma_start(stream[:], y_rows[:, : blocks * entries - half], max_dma_last_dim=2 * (blocks * entries - half))
         gates = [tile(places, f"gate{b}") for b in range(blocks)]
         for b in range(blocks):
             nc.sync.dma_start(gates[b][:], gate_rows[:, b, :])
@@ -53,7 +53,11 @@ def tile_lookup_vg_minrelu_out_kernel(tc, tab, y, offs, out):
         def gate_and_multiply(b, capped, product, first, end):
             opened = tile(end - first, f"opened{b}_{first}")
             nc.scalar.activation(opened[:], gates[b][:].indirect(listed(first, end)), RELU)
-            nc.vector.tensor_tensor(product[:, first:end], capped[:, first:end], opened[:], MULT)
+            nc.vector.tensor_tensor(product, capped[:, first:end], opened[:], MULT)
+
+        def gate_multiply_store(b, capped, product, first, end):
+            gate_and_multiply(b, capped, product, first, end)
+            nc.sync.dma_start(out_rows[:, b * entries + first : b * entries + end], product)
 
         cappeds = [tile(entries, f"capped{b}") for b in range(blocks)]
         for b in range(last):
@@ -62,16 +66,12 @@ def tile_lookup_vg_minrelu_out_kernel(tc, tab, y, offs, out):
         for b in range(last):
             product = tile(entries, f"product{b}")
             for first, end in [(0, half), (half, entries)] if b == last - 1 else [(0, entries)]:
-                gate_and_multiply(b, cappeds[b], product, first, end)
-                nc.sync.dma_start(out_rows[:, b, first:end], product[:, first:end])
+                gate_multiply_store(b, cappeds[b], product[:, first:end], first, end)
 
-        capped, product = cappeds[last], tile(entries, "product_last")
+        capped, product = cappeds[last], tile(half, "product_last")
+        quarter = entries // 4
         cap(last, capped, half, half + STEP, late[:, :STEP])
         cap(last, capped, half + STEP, entries, late[:, STEP:])
-        gate_and_multiply(last, capped, stream_end, 0, half)
-        nc.sync.dma_start(out_rows[:, last, :half], stream_end[:, :half])
-        cut = half + half // 2
-        gate_and_multiply(last, capped, product, half, cut)
-        nc.sync.dma_start(out_rows[:, last, half:cut], product[:, half:cut])
-        gate_and_multiply(last, capped, product, cut, entries)
-        nc.sync.dma_start(out_rows[:, last, cut:], product[:, cut:])
+        gate_multiply_store(last, capped, stream_end[:, :half], 0, half)
+        gate_multiply_store(last, capped, product[:, :quarter], half, half + quarter)
+        gate_multiply_store(last, capped, product[:, quarter:], half + quarter, entries)

@@ -5,6 +5,7 @@ MIN, MULT = mybir.AluOpType.min, mybir.AluOpType.mult
 RELU = mybir.ActivationFunctionType.Relu
 P = 128
 ALIGN = 256
+PIECE = 192
 STEP = 64
 
 
@@ -33,8 +34,8 @@ def tile_lookup_vg_minrelu_out_kernel(tc, tab, y, offs, out):
         gates = [tile(places, f"gate{b}") for b in range(blocks)]
         for b in range(blocks):
             nc.sync.dma_start(gates[b][:], gate_rows[:, b, :])
-        stream_end = tile(entries - STEP, "stream_end")
-        late = stream_end[:, half - STEP :]
+        stream_end = tile(PIECE - STEP + half, "stream_end")
+        late = stream_end[:, PIECE - STEP :]
         nc.sync.dma_start(late, y_rows[:, blocks * entries - half :])
 
         def listed(first, end):
@@ -68,10 +69,9 @@ def tile_lookup_vg_minrelu_out_kernel(tc, tab, y, offs, out):
             for first, end in [(0, half), (half, entries)] if b == last - 1 else [(0, entries)]:
                 gate_multiply_store(b, cappeds[b], product[:, first:end], first, end)
 
-        capped, product = cappeds[last], tile(half, "product_last")
-        quarter = entries // 4
+        capped, product = cappeds[last], tile(entries - PIECE, "product_last")
         cap(last, capped, half, half + STEP, late[:, :STEP])
         cap(last, capped, half + STEP, entries, late[:, STEP:])
-        gate_multiply_store(last, capped, stream_end[:, :half], 0, half)
-        gate_multiply_store(last, capped, product[:, :quarter], half, half + quarter)
-        gate_multiply_store(last, capped, product[:, quarter:], half + quarter, entries)
+        gate_multiply_store(last, capped, stream_end[:, :PIECE], 0, PIECE)
+        gate_multiply_store(last, capped, product[:, :PIECE], PIECE, 2 * PIECE)
+        gate_multiply_store(last, capped, product[:, PIECE:], 2 * PIECE, entries)

@@ -71,7 +71,8 @@ def tile_lookup_vg_minrelu_out_kernel(tc, tab, y, offs, out):
 
         capped, product = cappeds[last], tile(entries - PIECE, "product_last")
         cap(last, capped, half, half + STEP, late[:, :STEP])
-        cap(last, capped, half + STEP, entries, late[:, STEP:])
+        cap(last, capped, half + STEP, 2 * PIECE, late[:, STEP : 2 * PIECE - half])
         gate_multiply_store(last, capped, stream_end[:, :PIECE], 0, PIECE)
+        cap(last, capped, 2 * PIECE, entries, late[:, 2 * PIECE - half :])
         gate_multiply_store(last, capped, product[:, :PIECE], PIECE, 2 * PIECE)
         gate_multiply_store(last, capped, product[:, PIECE:], 2 * PIECE, entries)

@@ -30,9 +30,10 @@ def tile_lookup_vg_minrelu_out_kernel(tc, tab, y, offs, out):
         offsets = held.tile([P, entries // 16], U16, name="offsets")
         nc.sync.dma_start(offsets[:], offs)
         stream = tile(blocks * entries - half, "stream")
-        nc.scalar.dma_start(stream[:], y_rows[:, : blocks * entries - half], max_dma_last_dim=2 * (blocks * entries - half))
+        nc.scalar.dma_start(stream[:], y_rows[:, : blocks * entries - half])
         gates = [tile(places, f"gate{b}") for b in range(blocks)]
-        for b in range(blocks):
+        nc.scalar.dma_start(gates[0][:], gate_rows[:, 0, :])
+        for b in range(1, blocks):
             nc.sync.dma_start(gates[b][:], gate_rows[:, b, :])
         stream_end = tile(PIECE - STEP + half, "stream_end")
         late = stream_end[:, PIECE - STEP :]
@@ -66,7 +67,7 @@ def tile_lookup_vg_minrelu_out_kernel(tc, tab, y, offs, out):
         cap(last, cappeds[last], 0, half, stream[:, last * entries :])
         for b in range(last):
             product = tile(entries, f"product{b}")
-            for first, end in [(0, half), (half, entries)] if b == last - 1 else [(0, entries)]:
+            for first, end in [(0, half), (half, entries)] if b > 0 else [(0, entries)]:
                 gate_multiply_store(b, cappeds[b], product[:, first:end], first, end)
 
         capped, product = cappeds[last], tile(entries - PIECE, "product_last")

@@ -5,7 +5,6 @@ MIN, MULT = mybir.AluOpType.min, mybir.AluOpType.mult
 RELU = mybir.ActivationFunctionType.Relu
 P = 128
 ALIGN = 256
-PIECE = 192
 STEP = 64
 
 
@@ -15,7 +14,9 @@ def tile_lookup_vg_minrelu_out_kernel(tc, tab, y, offs, out):
     places = tab.shape[2]
     blocks = rows // P
     last = blocks - 1
-    half = entries // 2
+    half, quarter = entries // 2, entries // 4
+    piece = 3 * STEP
+    early = last * entries + quarter
     value_rows = tab[0].rearrange("(p b) s -> p (b s)", b=blocks)
     gate_rows = tab[1].rearrange("(p b) s -> p b s", b=blocks)
     y_rows = y.rearrange("(p b) j -> p (b j)", b=blocks)
@@ -29,15 +30,15 @@ def tile_lookup_vg_minrelu_out_kernel(tc, tab, y, offs, out):
         nc.sync.dma_start(all_values[:], value_rows)
         offsets = held.tile([P, entries // 16], U16, name="offsets")
         nc.sync.dma_start(offsets[:], offs)
-        stream = tile(blocks * entries - half, "stream")
-        nc.scalar.dma_start(stream[:], y_rows[:, : blocks * entries - half])
+        stream = tile(early, "stream")
+        nc.scalar.dma_start(stream[:], y_rows[:, :early])
         gates = [tile(places, f"gate{b}") for b in range(blocks)]
         nc.scalar.dma_start(gates[0][:], gate_rows[:, 0, :])
         for b in range(1, blocks):
             nc.sync.dma_start(gates[b][:], gate_rows[:, b, :])
-        stream_end = tile(PIECE - STEP + half, "stream_end")
-        late = stream_end[:, PIECE - STEP :]
-        nc.sync.dma_start(late, y_rows[:, blocks * entries - half :])
+        late = tile(entries - quarter, "late")
+        nc.sync.dma_start(late[:, :quarter], y_rows[:, early : early + quarter])
+        nc.sync.dma_start(late[:, quarter:], y_rows[:, early + quarter :])
 
         def listed(first, end):
             return offsets[:, first // 16 : end // 16]
@@ -49,31 +50,33 @@ def tile_lookup_vg_minrelu_out_kernel(tc, tab, y, offs, out):
             else:
                 nc.scalar.copy(values[b][:], all_values[:, b * places : (b + 1) * places])
 
-        def cap(b, capped, first, end, y_piece):
-            nc.vector.tensor_tensor(capped[:, first:end], values[b][:].indirect(listed(first, end)), y_piece, MIN)
+        cappeds = [tile(entries, f"capped{b}") for b in range(blocks)]
 
-        def gate_and_multiply(b, capped, product, first, end):
+        def cap(b, first, end, y_piece):
+            nc.vector.tensor_tensor(cappeds[b][:, first:end], values[b][:].indirect(listed(first, end)), y_piece, MIN)
+
+        def cap_late(first, end):
+            cap(last, first, end, late[:, first - quarter : end - quarter])
+
+        def gate_multiply_store(b, first, end, product):
             opened = tile(end - first, f"opened{b}_{first}")
             nc.scalar.activation(opened[:], gates[b][:].indirect(listed(first, end)), RELU)
-            nc.vector.tensor_tensor(product, capped[:, first:end], opened[:], MULT)
-
-        def gate_multiply_store(b, capped, product, first, end):
-            gate_and_multiply(b, capped, product, first, end)
+            nc.vector.tensor_tensor(product, cappeds[b][:, first:end], opened[:], MULT)
             nc.sync.dma_start(out_rows[:, b * entries + first : b * entries + end], product)
 
-        cappeds = [tile(entries, f"capped{b}") for b in range(blocks)]
         for b in range(last):
-            cap(b, cappeds[b], 0, entries, stream[:, b * entries : (b + 1) * entries])
-        cap(last, cappeds[last], 0, half, stream[:, last * entries :])
+            cap(b, 0, entries, stream[:, b * entries : (b + 1) * entries])
+        cap(last, 0, quarter, stream[:, last * entries :])
         for b in range(last):
             product = tile(entries, f"product{b}")
-            for first, end in [(0, half), (half, entries)] if b > 0 else [(0, entries)]:
-                gate_multiply_store(b, cappeds[b], product[:, first:end], first, end)
+            for first, end in [(0, half), (half, entries)] if b == last - 1 else [(0, entries)]:
+                gate_multiply_store(b, first, end, product[:, first:end])
 
-        capped, product = cappeds[last], tile(entries - PIECE, "product_last")
-        cap(last, capped, half, half + STEP, late[:, :STEP])
-        cap(last, capped, half + STEP, 2 * PIECE, late[:, STEP : 2 * PIECE - half])
-        gate_multiply_store(last, capped, stream_end[:, :PIECE], 0, PIECE)
-        cap(last, capped, 2 * PIECE, entries, late[:, 2 * PIECE - half :])
-        gate_multiply_store(last, capped, product[:, :PIECE], PIECE, 2 * PIECE)
-        gate_multiply_store(last, capped, product[:, PIECE:], 2 * PIECE, entries)
+        product = tile(entries - piece, "product_last")
+        cap_late(quarter, half)
+        cap_late(half, half + STEP)
+        cap_late(half + STEP, 2 * piece)
+        gate_multiply_store(last, 0, piece, late[:, :piece])
+        cap_late(2 * piece, entries)
+        gate_multiply_store(last, piece, 2 * piece, product[:, :piece])
+        gate_multiply_store(last, 2 * piece, entries, product[:, piece:])

@@ -14,9 +14,9 @@ def tile_lookup_vg_minrelu_out_kernel(tc, tab, y, offs, out):
     places = tab.shape[2]
     blocks = rows // P
     last = blocks - 1
-    half, quarter = entries // 2, entries // 4
+    half = entries // 2
     piece = 3 * STEP
-    early = last * entries + quarter
+    early = last * entries + piece
     value_rows = tab[0].rearrange("(p b) s -> p (b s)", b=blocks)
     gate_rows = tab[1].rearrange("(p b) s -> p b s", b=blocks)
     y_rows = y.rearrange("(p b) j -> p (b j)", b=blocks)
@@ -36,9 +36,9 @@ def tile_lookup_vg_minrelu_out_kernel(tc, tab, y, offs, out):
         nc.scalar.dma_start(gates[0][:], gate_rows[:, 0, :])
         for b in range(1, blocks):
             nc.sync.dma_start(gates[b][:], gate_rows[:, b, :])
-        late = tile(entries - quarter, "late")
-        nc.sync.dma_start(late[:, :quarter], y_rows[:, early : early + quarter])
-        nc.sync.dma_start(late[:, quarter:], y_rows[:, early + quarter :])
+        late = tile(entries - piece, "late")
+        nc.sync.dma_start(late[:, : 2 * STEP], y_rows[:, early : early + 2 * STEP])
+        nc.sync.dma_start(late[:, 2 * STEP :], y_rows[:, early + 2 * STEP :])
 
         def listed(first, end):
             return offsets[:, first // 16 : end // 16]
@@ -56,7 +56,7 @@ def tile_lookup_vg_minrelu_out_kernel(tc, tab, y, offs, out):
             nc.vector.tensor_tensor(cappeds[b][:, first:end], values[b][:].indirect(listed(first, end)), y_piece, MIN)
 
         def cap_late(first, end):
-            cap(last, first, end, late[:, first - quarter : end - quarter])
+            cap(last, first, end, late[:, first - piece : end - piece])
 
         def gate_multiply_store(b, first, end, product):
             opened = tile(end - first, f"opened{b}_{first}")
@@ -66,17 +66,17 @@ def tile_lookup_vg_minrelu_out_kernel(tc, tab, y, offs, out):
 
         for b in range(last):
             cap(b, 0, entries, stream[:, b * entries : (b + 1) * entries])
-        cap(last, 0, quarter, stream[:, last * entries :])
+        cap(last, 0, piece, stream[:, last * entries :])
         for b in range(last):
             product = tile(entries, f"product{b}")
             for first, end in [(0, half), (half, entries)] if b == last - 1 else [(0, entries)]:
                 gate_multiply_store(b, first, end, product[:, first:end])
 
         product = tile(entries - piece, "product_last")
-        cap_late(quarter, half)
-        cap_late(half, half + STEP)
-        cap_late(half + STEP, 2 * piece)
+        cap_late(piece, piece + 2 * STEP)
+        cap_late(piece + 2 * STEP, 2 * piece)
+        cap_late(2 * piece, entries - STEP)
         gate_multiply_store(last, 0, piece, late[:, :piece])
-        cap_late(2 * piece, entries)
+        cap_late(entries - STEP, entries)
         gate_multiply_store(last, piece, 2 * piece, product[:, :piece])
         gate_multiply_store(last, 2 * piece, entries, product[:, piece:])

import concourse.mybir as mybir

F32, U16 = mybir.dt.float32, mybir.dt.uint16
MIN, MULT = mybir.AluOpType.min, mybir.AluOpType.mult
RELU = mybir.ActivationFunctionType.Relu
P = 128
ALIGN = 256
STEP = 64


def tile_lookup_vg_minrelu_out_kernel(tc, tab, y, offs, out):
    nc = tc.nc
    rows, entries = y.shape
    places = tab.shape[2]
    blocks = rows // P
    last = blocks - 1
    half = entries // 2
    piece = 3 * STEP
    early = last * entries + piece
    value_rows = tab[0].rearrange("(p b) s -> p (b s)", b=blocks)
    gate_rows = tab[1].rearrange("(p b) s -> p b s", b=blocks)
    y_rows = y.rearrange("(p b) j -> p (b j)", b=blocks)
    out_rows = out.rearrange("(p b) j -> p (b j)", b=blocks)
    with tc.tile_pool(name="held", bufs=1) as held:

        def tile(columns, name):
            return held.tile([P, columns], F32, name=name, align_bytes=ALIGN)

        all_values = tile(blocks * places, "all_values")
        nc.sync.dma_start(all_values[:], value_rows)
        offsets = held.tile([P, entries // 16], U16, name="offsets")
        nc.sync.dma_start(offsets[:], offs)
        stream = tile(early, "stream")
        nc.scalar.dma_start(stream[:], y_rows[:, :early])
        gates = [tile(places, f"gate{b}") for b in range(blocks)]
        nc.scalar.dma_start(gates[0][:], gate_rows[:, 0, :])
        for b in range(1, blocks):
            nc.sync.dma_start(gates[b][:], gate_rows[:, b, :])
        late = tile(entries - piece, "late")
        nc.sync.dma_start(late[:, : 2 * STEP], y_rows[:, early : early + 2 * STEP])
        nc.sync.dma_start(late[:, 2 * STEP :], y_rows[:, early + 2 * STEP :])

        def listed(first, end):
            return offsets[:, first // 16 : end // 16]

        values = [tile(places, f"value{b}") for b in range(blocks)]
        for b in range(blocks):
            if b < blocks // 2:
                nc.vector.tensor_copy(values[b][:], all_values[:, b * places : (b + 1) * places])
            else:
                nc.scalar.copy(values[b][:], all_values[:, b * places : (b + 1) * places])

        cappeds = [tile(entries, f"capped{b}") for b in range(blocks)]

        def cap(b, first, end, y_piece):
            nc.vector.tensor_tensor(cappeds[b][:, first:end], values[b][:].indirect(listed(first, end)), y_piece, MIN)

        def cap_late(first, end):
            cap(last, first, end, late[:, first - piece : end - piece])

        def gate_multiply_store(b, first, end, product):
            opened = tile(end - first, f"opened{b}_{first}")
            nc.scalar.activation(opened[:], gates[b][:].indirect(listed(first, end)), RELU)
            nc.vector.tensor_tensor(product, cappeds[b][:, first:end], opened[:], MULT)
            nc.sync.dma_start(out_rows[:, b * entries + first : b * entries + end], product)

        for b in range(last):
            cap(b, 0, entries, stream[:, b * entries : (b + 1) * entries])
        cap(last, 0, piece, stream[:, last * entries :])
        for b in range(last):
            product = tile(entries, f"product{b}")
            for first, end in [(0, half), (half, entries)] if b == last - 1 else [(0, entries)]:
                gate_multiply_store(b, first, end, product[:, first:end])

        product = tile(entries - piece, "product_last")
        cap_late(piece, piece + 2 * STEP)
        cap_late(piece + 2 * STEP, 2 * piece)
        cap_late(2 * piece, entries - STEP)
        gate_multiply_store(last, 0, piece, late[:, :piece])
        cap_late(entries - STEP, entries)
        gate_multiply_store(last, piece, 2 * piece, product[:, :piece])
        gate_multiply_store(last, 2 * piece, entries, product[:, piece:])
